import numpy as np
import ml_dtypes


def mxq(x, axis, fmt="e4m3"):
    dtype, down = {"e4m3": (ml_dtypes.float8_e4m3fn, 7), "e5m2": (ml_dtypes.float8_e5m2, 14)}[fmt]
    v = np.moveaxis(np.asarray(x, np.float32).astype(ml_dtypes.bfloat16).astype(np.float64), axis, -1)
    blocks = v.reshape(v.shape[:-1] + (-1, 32))
    amax = np.abs(blocks).max(-1, keepdims=True)
    byte = np.maximum(np.where(amax > 0, np.frexp(amax)[1] - 1 + 127, 0) - down, 1)
    scale = np.exp2(byte - 127.0)
    codes = (blocks / scale).astype(np.float32).astype(dtype).astype(np.float64)
    return np.moveaxis((codes * scale).reshape(v.shape), -1, axis)


WIDE = False


def mx_kscale(k):
    if not WIDE:
        return np.ones(k)
    levels = np.array([10, -10, 5, -5, 0])
    if k % 512:
        return np.exp2(np.random.permutation(np.resize(levels, k // 32))).repeat(32)
    a = np.empty((k // 512, 16))
    for p in range(k // 512):
        a[p, :8] = np.random.permutation(np.resize(levels, 8))
        for g in range(8):
            far = levels[np.abs(levels - a[p, g]) >= 10]
            a[p, g + 8] = far[np.random.randint(len(far))]
    return np.exp2(a.ravel()).repeat(32)


def f64(x):
    return np.asarray(x).astype(np.float64)


def striped(idx):
    return np.tile(idx.reshape(-1, 16).T, (8, 1)).astype(np.uint16)


def unstriped(offs):
    return offs[:16].T.reshape(-1).astype(np.int64)


def pack_weight(w):
    k, n = w.shape
    w = f64(np.asarray(w, np.float32).astype(ml_dtypes.bfloat16)).reshape(k // 32, 32, n)
    amax = np.abs(w).max(1)
    byte = np.clip(np.where(amax > 0, np.frexp(amax)[1] - 1 + 127 - 7, 1), 1, 254)
    scaled = (w * np.exp2(127.0 - byte)[:, None, :]).reshape(k, n).astype(np.float32)
    words = np.ascontiguousarray(scaled.reshape(k // 512, 128, 4, n).transpose(0, 1, 3, 2)).astype(ml_dtypes.float8_e4m3fn).view(np.uint8)
    return words, np.ascontiguousarray(byte.astype(np.uint8).reshape(k // 512, 16, n))


def unpack_weight(words, scales):
    g, p, n, _ = words.shape
    vals = np.ascontiguousarray(words).view(ml_dtypes.float8_e4m3fn).astype(np.float64) * np.repeat(np.exp2(scales.astype(np.float64) - 127.0), 8, axis=1)[..., None]
    return vals.transpose(0, 1, 3, 2).reshape(g * 512, n)


def relu2(v):
    return np.maximum(v, 0.0) ** 2


K, T, S, N = 2048, 1024, 512, 128


def setup_inputs():
    n = np.random.standard_normal
    s = mx_kscale(K)[:, None]
    words, scales = pack_weight(n((K, N)) / np.sqrt(K) / s)
    return {
        "xT": (n((K, T)) * s).astype(np.float32),
        "w_words": words,
        "w_scales": scales,
        "b": (0.3 * n((N, 1))).astype(np.float32),
        "offs": striped(np.sort(np.random.permutation(T)[:S])),
    }


def reference(xT, w_words, w_scales, b, offs):
    w = unpack_weight(w_words, w_scales)
    idx = unstriped(offs)
    xq = mxq(f64(xT)[:, idx], 0, "e4m3")
    y = w.T @ xq
    y = relu2(y + f64(b))
    return y

@@ -1,0 +1,130 @@
+from contextlib import ExitStack
+
+import concourse.mybir as mybir
+
+K, T, S, N = 2048, 1024, 512, 128
+FLOPS = 2 * K * S * N
+
+F32 = mybir.dt.float32
+BF16 = mybir.dt.bfloat16
+I32 = mybir.dt.int32
+U32 = mybir.dt.uint32
+U16 = mybir.dt.uint16
+U8 = mybir.dt.uint8
+FP8X4 = mybir.dt.float8_e4m3fn_x4
+RELU = mybir.ActivationFunctionType.Relu
+SQUARE = mybir.ActivationFunctionType.Square
+ADD, MAX, MULT = mybir.AluOpType.add, mybir.AluOpType.max, mybir.AluOpType.mult
+
+P = 128
+PASSES = K // 512
+HALF = S // 2
+
+
+def tile_picked_pick_lin_relu2_srt_e_kernel(tc, xT, w_words, w_scales, b, offs, out):
+    nc = tc.nc
+    x_rows = xT.rearrange("(a p j) t -> a p j t", p=P, j=4)
+
+    with ExitStack() as ctx:
+        keep = ctx.enter_context(tc.tile_pool(name="keep", bufs=1))
+        psum = ctx.enter_context(tc.psum_pool(name="psum", bufs=1))
+
+        offsets = keep.tile([P, S // 16], U16, name="offsets")
+        bias = keep.tile([P, 1], F32, name="bias")
+        w_codes = keep.tile([P, PASSES, N], U32, align_bytes=64, name="w_codes")
+        w_scale = keep.tile([P, PASSES, N], U8, align_bytes=64, name="w_scale")
+        warm = keep.tile([P, 1], F32, name="warm")
+        warmed = keep.tile([P, 1], F32, name="warmed")
+
+        nc.vector.memset(w_scale[:].rearrange("p a n -> p (a n)").bitcast(I32), 0)
+        nc.vector.memset(warm[:], 0.0)
+        nc.scalar.activation(out=warmed[:], in_=warm[:], func=RELU)
+
+        pairs = [(a, u) for a in range(PASSES) for u in range(2)]
+        cuts = {0: [0, 512, T], 7: [0, 512, 896, T]}
+        raw = []
+        for i, (a, u) in enumerate(pairs):
+            x = keep.tile([P, 2, T], F32, name=f"x{i}")
+            raw.append(x)
+            if i == 7:
+                nc.sync.dma_start(out=w_codes[:].bitcast(I32), in_=w_words.rearrange("a p n r -> p a (n r)").bitcast(I32))
+            edges = cuts.get(i, [0, T])
+            for c, (lo, hi) in enumerate(zip(edges[:-1], edges[1:])):
+                nc.sync.dma_start(out=x[:, :, lo:hi], in_=x_rows[a][:, 2 * u : 2 * u + 2, lo:hi])
+                if i == 0 and c == 0:
+                    nc.sync.dma_start(offsets[:], offs)
+            if i == 1:
+                nc.sync.dma_start(out=bias[:], in_=b)
+            if i == 2:
+                for q in range(4):
+                    nc.sync.dma_start(
+                        out=w_scale[32 * q : 32 * q + 4].bitcast(I32),
+                        in_=w_scales[:, 4 * q : 4 * q + 4, :].rearrange("a q n -> q a n").bitcast(I32),
+                    )
+
+        acc = []
+        for h in range(2):
+            bank = psum.tile([P, HALF], F32, name=f"acc{h}")
+            acc.append(bank)
+
+        def cast(i, pair, engine, lo, hi):
+            src = raw[i][:, :, lo:hi].rearrange("p e t -> p t e")
+            if engine == "s":
+                nc.scalar.copy(out=pair[:, lo:hi, :], in_=src)
+            else:
+                nc.vector.tensor_copy(out=pair[:, lo:hi, :], in_=src)
+
+        plan = {
+            0: [("s", 0, 176), ("v", 176, 512), ("s", 512, 688), ("v", 688, T)],
+            6: [("s", 0, 640), ("v", 640, T)],
+            7: [("s", 0, 512), ("v", 512, 896), ("v", 896, T)],
+        }
+        grouped = None
+        for i, (a, u) in enumerate(pairs):
+            pair = keep.tile([P, T, 2], BF16, name=f"pair{i}")
+            for engine, lo, hi in plan.get(i, [("s", 0, 832), ("v", 832, T)]):
+                cast(i, pair, engine, lo, hi)
+            window = pair[:].rearrange("p t e -> p (t e)").bitcast(U32)
+            if u == 0:
+                grouped = keep.tile([P, S, 4], BF16, align_bytes=64, name=f"grouped{a}")
+                codes = keep.tile([P, S], U32, align_bytes=64, name=f"codes{a}")
+                scale = keep.tile([P, S], U8, align_bytes=64, name=f"scale{a}")
+            flat = grouped[:].rearrange("p s k -> p (s k)")
+            words = flat.bitcast(U32).rearrange("p (s u) -> p s u", u=2)
+            last = a == PASSES - 1
+            if i == 7:
+                for h in range(2):
+                    nc.vector.tensor_copy(
+                        out=words[:, h * HALF : (h + 1) * HALF, u],
+                        in_=window.indirect(offsets[:, h * HALF // 16 : (h + 1) * HALF // 16]),
+                    )
+            else:
+                nc.vector.tensor_copy(out=words[:, :, u], in_=window.indirect(offsets[:]))
+            if u == 1:
+                slices = [(0, HALF), (HALF, S)] if last else [(0, S)]
+                for lo, hi in slices:
+                    nc.vector.quantize_mx(
+                        out=codes[:, lo:hi].bitcast(FP8X4), scales=scale[:, lo:hi], in_=flat[:, 4 * lo : 4 * hi]
+                    )
+                for h in range(2):
+                    cols = slice(h * HALF, (h + 1) * HALF)
+                    nc.tensor.matmul_mx(
+                        out=acc[h][:],
+                        lhsT=w_codes[:, a, :].bitcast(FP8X4),
+                        lhsT_scale=w_scale[:, a, :],
+                        rhs=codes[:, cols].bitcast(FP8X4),
+                        rhs_scale=scale[:, cols],
+                        start=(a == 0),
+                        stop=last,
+                    )
+
+        for h in range(2):
+            relu = keep.tile([P, HALF], F32, name=f"relu{h}")
+            y = keep.tile([P, HALF], F32, name=f"y{h}")
+            if h == 0:
+                nc.scalar.activation(out=relu[:], in_=acc[h][:], func=RELU, bias=bias[:])
+                nc.scalar.activation(out=y[:], in_=relu[:], func=SQUARE)
+            else:
+                nc.vector.tensor_scalar(out=relu[:], in0=acc[h][:], scalar1=bias[:], scalar2=0.0, op0=ADD, op1=MAX)
+                nc.vector.tensor_tensor(out=y[:], in0=relu[:], in1=relu[:], op=MULT)
+            nc.sync.dma_start(out=out[:, h * HALF : (h + 1) * HALF], in_=y[:])

@@ -38,6 +38,12 @@ def tile_picked_pick_lin_relu2_srt_e_kernel(tc, xT, w_words, w_scales, b, offs, 
 
         nc.vector.memset(w_scale[:].rearrange("p a n -> p (a n)").bitcast(I32), 0)
         nc.vector.memset(warm[:], 0.0)
+        nc.scalar.dma_start(out=bias[:], in_=b)
+        for q in range(4):
+            nc.scalar.dma_start(
+                out=w_scale[32 * q : 32 * q + 4].bitcast(I32),
+                in_=w_scales[:, 4 * q : 4 * q + 4, :].rearrange("a q n -> q a n").bitcast(I32),
+            )
         nc.scalar.activation(out=warmed[:], in_=warm[:], func=RELU)
 
         pairs = [(a, u) for a in range(PASSES) for u in range(2)]
@@ -53,18 +59,11 @@ def tile_picked_pick_lin_relu2_srt_e_kernel(tc, xT, w_words, w_scales, b, offs, 
                 nc.sync.dma_start(out=x[:, :, lo:hi], in_=x_rows[a][:, 2 * u : 2 * u + 2, lo:hi])
                 if i == 0 and c == 0:
                     nc.sync.dma_start(offsets[:], offs)
-            if i == 1:
-                nc.sync.dma_start(out=bias[:], in_=b)
-            if i == 2:
-                for q in range(4):
-                    nc.sync.dma_start(
-                        out=w_scale[32 * q : 32 * q + 4].bitcast(I32),
-                        in_=w_scales[:, 4 * q : 4 * q + 4, :].rearrange("a q n -> q a n").bitcast(I32),
-                    )
 
+        parts = [(0, 256), (256, 384), (384, 512)]
         acc = []
-        for h in range(2):
-            bank = psum.tile([P, HALF], F32, name=f"acc{h}")
+        for h, (lo, hi) in enumerate(parts):
+            bank = psum.tile([P, 512], F32, name=f"acc{h}")
             acc.append(bank)
 
         def cast(i, pair, engine, lo, hi):
@@ -76,7 +75,7 @@ def tile_picked_pick_lin_relu2_srt_e_kernel(tc, xT, w_words, w_scales, b, offs, 
 
         plan = {
             0: [("s", 0, 176), ("v", 176, 512), ("s", 512, 688), ("v", 688, T)],
-            6: [("s", 0, 640), ("v", 640, T)],
+            6: [("s", 0, 560), ("v", 560, T)],
             7: [("s", 0, 512), ("v", 512, 896), ("v", 896, T)],
         }
         grouped = None
@@ -86,30 +85,30 @@ def tile_picked_pick_lin_relu2_srt_e_kernel(tc, xT, w_words, w_scales, b, offs, 
                 cast(i, pair, engine, lo, hi)
             window = pair[:].rearrange("p t e -> p (t e)").bitcast(U32)
             if u == 0:
+                gathered = keep.tile([P, 2, S, 2], BF16, align_bytes=64, name=f"gathered{a}")
                 grouped = keep.tile([P, S, 4], BF16, align_bytes=64, name=f"grouped{a}")
                 codes = keep.tile([P, S], U32, align_bytes=64, name=f"codes{a}")
                 scale = keep.tile([P, S], U8, align_bytes=64, name=f"scale{a}")
+            words = gathered[:, u].rearrange("p s e -> p (s e)").bitcast(U32)
             flat = grouped[:].rearrange("p s k -> p (s k)")
-            words = flat.bitcast(U32).rearrange("p (s u) -> p s u", u=2)
             last = a == PASSES - 1
-            if i == 7:
-                for h in range(2):
-                    nc.vector.tensor_copy(
-                        out=words[:, h * HALF : (h + 1) * HALF, u],
-                        in_=window.indirect(offsets[:, h * HALF // 16 : (h + 1) * HALF // 16]),
-                    )
-            else:
-                nc.vector.tensor_copy(out=words[:, :, u], in_=window.indirect(offsets[:]))
+            for lo, hi in [(0, HALF), (HALF, S)] if i == 7 else [(0, S)]:
+                nc.vector.tensor_copy(out=words[:, lo:hi], in_=window.indirect(offsets[:, lo // 16 : hi // 16]))
             if u == 1:
                 slices = [(0, HALF), (HALF, S)] if last else [(0, S)]
+                for lo, hi in slices:
+                    nc.vector.tensor_copy(
+                        out=grouped[:, lo:hi].rearrange("p s (u e) -> p s u e", u=2),
+                        in_=gathered[:, :, lo:hi].rearrange("p u s e -> p s u e"),
+                    )
                 for lo, hi in slices:
                     nc.vector.quantize_mx(
                         out=codes[:, lo:hi].bitcast(FP8X4), scales=scale[:, lo:hi], in_=flat[:, 4 * lo : 4 * hi]
                     )
-                for h in range(2):
-                    cols = slice(h * HALF, (h + 1) * HALF)
+                for h, (lo, hi) in enumerate(parts):
+                    cols = slice(lo, hi)
                     nc.tensor.matmul_mx(
-                        out=acc[h][:],
+                        out=acc[h][:, : hi - lo],
                         lhsT=w_codes[:, a, :].bitcast(FP8X4),
                         lhsT_scale=w_scale[:, a, :],
                         rhs=codes[:, cols].bitcast(FP8X4),
@@ -118,13 +117,14 @@ def tile_picked_pick_lin_relu2_srt_e_kernel(tc, xT, w_words, w_scales, b, offs, 
                         stop=last,
                     )
 
-        for h in range(2):
-            relu = keep.tile([P, HALF], F32, name=f"relu{h}")
-            y = keep.tile([P, HALF], F32, name=f"y{h}")
-            if h == 0:
-                nc.scalar.activation(out=relu[:], in_=acc[h][:], func=RELU, bias=bias[:])
-                nc.scalar.activation(out=y[:], in_=relu[:], func=SQUARE)
-            else:
-                nc.vector.tensor_scalar(out=relu[:], in0=acc[h][:], scalar1=bias[:], scalar2=0.0, op0=ADD, op1=MAX)
+        for h, (lo, hi) in enumerate(parts):
+            relu = keep.tile([P, hi - lo], F32, name=f"relu{h}")
+            y = keep.tile([P, hi - lo], F32, name=f"y{h}")
+            total = acc[h][:, : hi - lo]
+            if h == 1:
+                nc.vector.tensor_scalar(out=relu[:], in0=total, scalar1=bias[:], scalar2=0.0, op0=ADD, op1=MAX)
                 nc.vector.tensor_tensor(out=y[:], in0=relu[:], in1=relu[:], op=MULT)
-            nc.sync.dma_start(out=out[:, h * HALF : (h + 1) * HALF], in_=y[:])
+            else:
+                nc.scalar.activation(out=relu[:], in_=total, func=RELU, bias=bias[:])
+                nc.scalar.activation(out=y[:], in_=relu[:], func=SQUARE)
+            nc.sync.dma_start(out=out[:, lo:hi], in_=y[:])

@@ -18,7 +18,7 @@ ADD, MAX, MULT = mybir.AluOpType.add, mybir.AluOpType.max, mybir.AluOpType.mult
 
 P = 128
 PASSES = K // 512
-HALF = S // 2
+PIECES = [(0, 128), (128, 384), (384, 512)]
 
 
 def tile_picked_pick_lin_relu2_srt_e_kernel(tc, xT, w_words, w_scales, b, offs, out):
@@ -47,42 +47,36 @@ def tile_picked_pick_lin_relu2_srt_e_kernel(tc, xT, w_words, w_scales, b, offs, 
         nc.scalar.activation(out=warmed[:], in_=warm[:], func=RELU)
 
         pairs = [(a, u) for a in range(PASSES) for u in range(2)]
-        cuts = {0: [0, 512, T], 7: [0, 512, 896, T]}
+        cuts = {0: [0, 512, T], 7: [0, 640, 896, T]}
         raw = []
         for i, (a, u) in enumerate(pairs):
             x = keep.tile([P, 2, T], F32, name=f"x{i}")
             raw.append(x)
-            if i == 7:
-                nc.sync.dma_start(out=w_codes[:].bitcast(I32), in_=w_words.rearrange("a p n r -> p a (n r)").bitcast(I32))
             edges = cuts.get(i, [0, T])
             for c, (lo, hi) in enumerate(zip(edges[:-1], edges[1:])):
                 nc.sync.dma_start(out=x[:, :, lo:hi], in_=x_rows[a][:, 2 * u : 2 * u + 2, lo:hi])
                 if i == 0 and c == 0:
                     nc.sync.dma_start(offsets[:], offs)
+        nc.sync.dma_start(out=w_codes[:].bitcast(I32), in_=w_words.rearrange("a p n r -> p a (n r)").bitcast(I32))
 
-        parts = [(0, 256), (256, 384), (384, 512)]
         acc = []
-        for h, (lo, hi) in enumerate(parts):
+        for h in range(3):
             bank = psum.tile([P, 512], F32, name=f"acc{h}")
             acc.append(bank)
 
-        def cast(i, pair, engine, lo, hi):
-            src = raw[i][:, :, lo:hi].rearrange("p e t -> p t e")
-            if engine == "s":
-                nc.scalar.copy(out=pair[:, lo:hi, :], in_=src)
-            else:
-                nc.vector.tensor_copy(out=pair[:, lo:hi, :], in_=src)
-
         plan = {
-            0: [("s", 0, 176), ("v", 176, 512), ("s", 512, 688), ("v", 688, T)],
-            6: [("s", 0, 560), ("v", 560, T)],
-            7: [("s", 0, 512), ("v", 512, 896), ("v", 896, T)],
+            0: [("s", 0, 192), ("v", 192, 512), ("s", 512, 704), ("v", 704, T)],
+            1: [("s", 0, 448), ("v", 448, T)],
+            7: [("s", 0, 576), ("v", 576, 640), ("s", 640, 768), ("v", 768, 896), ("v", 896, T)],
         }
-        grouped = None
         for i, (a, u) in enumerate(pairs):
             pair = keep.tile([P, T, 2], BF16, name=f"pair{i}")
-            for engine, lo, hi in plan.get(i, [("s", 0, 832), ("v", 832, T)]):
-                cast(i, pair, engine, lo, hi)
+            for engine, lo, hi in plan.get(i, [("s", 0, 640), ("v", 640, T)]):
+                src = raw[i][:, :, lo:hi].rearrange("p e t -> p t e")
+                if engine == "s":
+                    nc.scalar.copy(out=pair[:, lo:hi, :], in_=src)
+                else:
+                    nc.vector.tensor_copy(out=pair[:, lo:hi, :], in_=src)
             window = pair[:].rearrange("p t e -> p (t e)").bitcast(U32)
             if u == 0:
                 gathered = keep.tile([P, 2, S, 2], BF16, align_bytes=64, name=f"gathered{a}")
@@ -92,32 +86,55 @@ def tile_picked_pick_lin_relu2_srt_e_kernel(tc, xT, w_words, w_scales, b, offs, 
             words = gathered[:, u].rearrange("p s e -> p (s e)").bitcast(U32)
             flat = grouped[:].rearrange("p s k -> p (s k)")
             last = a == PASSES - 1
-            for lo, hi in [(0, HALF), (HALF, S)] if i == 7 else [(0, S)]:
-                nc.vector.tensor_copy(out=words[:, lo:hi], in_=window.indirect(offsets[:, lo // 16 : hi // 16]))
+
+            def gather(lo, hi):
+                nc.vector.tensor_copy(
+                    out=words[:, lo:hi],
+                    in_=window[:, 0 : T - S + hi].indirect(offsets[:, lo // 16 : hi // 16]),
+                )
+
+            def interleave(lo, hi):
+                nc.vector.tensor_copy(
+                    out=grouped[:, lo:hi].rearrange("p s (u e) -> p s u e", u=2),
+                    in_=gathered[:, :, lo:hi].rearrange("p u s e -> p s u e"),
+                )
+
+            def quantise(lo, hi):
+                nc.vector.quantize_mx(
+                    out=codes[:, lo:hi].bitcast(FP8X4), scales=scale[:, lo:hi], in_=flat[:, 4 * lo : 4 * hi]
+                )
+
+            if i < 7:
+                gather(0, S)
+                if u == 1:
+                    halves = [(0, 256), (256, 512)] if a == 2 else [(0, 512)]
+                    for lo, hi in halves:
+                        interleave(lo, hi)
+                    for lo, hi in halves:
+                        quantise(lo, hi)
+            else:
+                gather(*PIECES[0])
+                gather(*PIECES[1])
+                interleave(*PIECES[0])
+                gather(*PIECES[2])
+                interleave(*PIECES[1])
+                quantise(*PIECES[0])
+                interleave(*PIECES[2])
+                quantise(*PIECES[1])
+                quantise(*PIECES[2])
             if u == 1:
-                slices = [(0, HALF), (HALF, S)] if last else [(0, S)]
-                for lo, hi in slices:
-                    nc.vector.tensor_copy(
-                        out=grouped[:, lo:hi].rearrange("p s (u e) -> p s u e", u=2),
-                        in_=gathered[:, :, lo:hi].rearrange("p u s e -> p s u e"),
-                    )
-                for lo, hi in slices:
-                    nc.vector.quantize_mx(
-                        out=codes[:, lo:hi].bitcast(FP8X4), scales=scale[:, lo:hi], in_=flat[:, 4 * lo : 4 * hi]
-                    )
-                for h, (lo, hi) in enumerate(parts):
-                    cols = slice(lo, hi)
+                for h, (lo, hi) in enumerate(PIECES):
                     nc.tensor.matmul_mx(
                         out=acc[h][:, : hi - lo],
                         lhsT=w_codes[:, a, :].bitcast(FP8X4),
                         lhsT_scale=w_scale[:, a, :],
-                        rhs=codes[:, cols].bitcast(FP8X4),
-                        rhs_scale=scale[:, cols],
+                        rhs=codes[:, lo:hi].bitcast(FP8X4),
+                        rhs_scale=scale[:, lo:hi],
                         start=(a == 0),
                         stop=last,
                     )
 
-        for h, (lo, hi) in enumerate(parts):
+        for h, (lo, hi) in enumerate(PIECES):
             relu = keep.tile([P, hi - lo], F32, name=f"relu{h}")
             y = keep.tile([P, hi - lo], F32, name=f"y{h}")
             total = acc[h][:, : hi - lo]

@@ -19,6 +19,7 @@ ADD, MAX, MULT = mybir.AluOpType.add, mybir.AluOpType.max, mybir.AluOpType.mult
 P = 128
 PASSES = K // 512
 PIECES = [(0, 128), (128, 384), (384, 512)]
+GROUPS = [(0, 128), (128, 256), (256, 384), (384, 512)]
 
 
 def tile_picked_pick_lin_relu2_srt_e_kernel(tc, xT, w_words, w_scales, b, offs, out):
@@ -57,24 +58,32 @@ def tile_picked_pick_lin_relu2_srt_e_kernel(tc, xT, w_words, w_scales, b, offs, 
                 nc.sync.dma_start(out=x[:, :, lo:hi], in_=x_rows[a][:, 2 * u : 2 * u + 2, lo:hi])
                 if i == 0 and c == 0:
                     nc.sync.dma_start(offsets[:], offs)
-        nc.sync.dma_start(out=w_codes[:].bitcast(I32), in_=w_words.rearrange("a p n r -> p a (n r)").bitcast(I32))
+            if i >= 6:
+                some = slice(2 * (i - 6), 2 * (i - 5))
+                nc.sync.dma_start(
+                    out=w_codes[:, some].bitcast(I32), in_=w_words[some].rearrange("a p n r -> p a (n r)").bitcast(I32)
+                )
 
         acc = []
-        for h in range(3):
+        for h in range(4):
             bank = psum.tile([P, 512], F32, name=f"acc{h}")
             acc.append(bank)
 
         plan = {
             0: [("s", 0, 192), ("v", 192, 512), ("s", 512, 704), ("v", 704, T)],
-            1: [("s", 0, 448), ("v", 448, T)],
-            7: [("s", 0, 576), ("v", 576, 640), ("s", 640, 768), ("v", 768, 896), ("v", 896, T)],
+            6: [("s", 0, 768), ("g", 768, T)],
+            7: [("s", 0, 640), ("s", 640, 704), ("g", 704, 896), ("v", 896, T)],
         }
         for i, (a, u) in enumerate(pairs):
             pair = keep.tile([P, T, 2], BF16, name=f"pair{i}")
-            for engine, lo, hi in plan.get(i, [("s", 0, 640), ("v", 640, T)]):
+            for engine, lo, hi in plan.get(i, [("s", 0, 640), ("g", 640, T)]):
                 src = raw[i][:, :, lo:hi].rearrange("p e t -> p t e")
                 if engine == "s":
                     nc.scalar.copy(out=pair[:, lo:hi, :], in_=src)
+                elif engine == "g":
+                    nc.gpsimd.tensor_scalar(
+                        out=pair[:, lo:hi, :], in0=src, scalar1=1.0, scalar2=0.0, op0=MULT, op1=ADD
+                    )
                 else:
                     nc.vector.tensor_copy(out=pair[:, lo:hi, :], in_=src)
             window = pair[:].rearrange("p t e -> p (t e)").bitcast(U32)
@@ -93,11 +102,11 @@ def tile_picked_pick_lin_relu2_srt_e_kernel(tc, xT, w_words, w_scales, b, offs, 
                     in_=window[:, 0 : T - S + hi].indirect(offsets[:, lo // 16 : hi // 16]),
                 )
 
+            both = flat.bitcast(F32).rearrange("p (s u) -> p s u", u=2)
+            apart = gathered[:].rearrange("p u s e -> p (u s e)").bitcast(F32).rearrange("p (u s) -> p s u", u=2)
+
             def interleave(lo, hi):
-                nc.vector.tensor_copy(
-                    out=grouped[:, lo:hi].rearrange("p s (u e) -> p s u e", u=2),
-                    in_=gathered[:, :, lo:hi].rearrange("p u s e -> p s u e"),
-                )
+                nc.vector.tensor_copy(out=both[:, lo:hi], in_=apart[:, lo:hi])
 
             def quantise(lo, hi):
                 nc.vector.quantize_mx(
@@ -105,9 +114,10 @@ def tile_picked_pick_lin_relu2_srt_e_kernel(tc, xT, w_words, w_scales, b, offs, 
                 )
 
             if i < 7:
-                gather(0, S)
+                halves = [(0, 256), (256, 512)] if i == 5 else [(0, 512)]
+                for lo, hi in halves:
+                    gather(lo, hi)
                 if u == 1:
-                    halves = [(0, 256), (256, 512)] if a == 2 else [(0, 512)]
                     for lo, hi in halves:
                         interleave(lo, hi)
                     for lo, hi in halves:
@@ -115,15 +125,16 @@ def tile_picked_pick_lin_relu2_srt_e_kernel(tc, xT, w_words, w_scales, b, offs, 
             else:
                 gather(*PIECES[0])
                 gather(*PIECES[1])
+                lo, hi = PIECES[1]
+                nc.scalar.copy(out=both[:, lo:hi], in_=apart[:, lo:hi])
                 interleave(*PIECES[0])
                 gather(*PIECES[2])
-                interleave(*PIECES[1])
                 quantise(*PIECES[0])
                 interleave(*PIECES[2])
                 quantise(*PIECES[1])
                 quantise(*PIECES[2])
             if u == 1:
-                for h, (lo, hi) in enumerate(PIECES):
+                for h, (lo, hi) in enumerate(GROUPS):
                     nc.tensor.matmul_mx(
                         out=acc[h][:, : hi - lo],
                         lhsT=w_codes[:, a, :].bitcast(FP8X4),
@@ -134,11 +145,11 @@ def tile_picked_pick_lin_relu2_srt_e_kernel(tc, xT, w_words, w_scales, b, offs, 
                         stop=last,
                     )
 
-        for h, (lo, hi) in enumerate(PIECES):
+        for h, (lo, hi) in enumerate(GROUPS):
             relu = keep.tile([P, hi - lo], F32, name=f"relu{h}")
             y = keep.tile([P, hi - lo], F32, name=f"y{h}")
             total = acc[h][:, : hi - lo]
-            if h == 1:
+            if h % 2 == 1:
                 nc.vector.tensor_scalar(out=relu[:], in0=total, scalar1=bias[:], scalar2=0.0, op0=ADD, op1=MAX)
                 nc.vector.tensor_tensor(out=y[:], in0=relu[:], in1=relu[:], op=MULT)
             else:

@@ -33,22 +33,21 @@ def tile_picked_pick_lin_relu2_srt_e_kernel(tc, xT, w_words, w_scales, b, offs, 
         offsets = keep.tile([P, S // 16], U16, name="offsets")
         bias = keep.tile([P, 1], F32, name="bias")
         w_codes = keep.tile([P, PASSES, N], U32, align_bytes=64, name="w_codes")
-        w_scale = keep.tile([P, PASSES, N], U8, align_bytes=64, name="w_scale")
+        w_scale = keep.tile([P, N], U8, align_bytes=64, name="w_scale")
         warm = keep.tile([P, 1], F32, name="warm")
         warmed = keep.tile([P, 1], F32, name="warmed")
 
-        nc.vector.memset(w_scale[:].rearrange("p a n -> p (a n)").bitcast(I32), 0)
+        nc.vector.memset(w_scale[:].bitcast(I32), 0)
         nc.vector.memset(warm[:], 0.0)
         nc.scalar.dma_start(out=bias[:], in_=b)
         for q in range(4):
             nc.scalar.dma_start(
-                out=w_scale[32 * q : 32 * q + 4].bitcast(I32),
-                in_=w_scales[:, 4 * q : 4 * q + 4, :].rearrange("a q n -> q a n").bitcast(I32),
+                out=w_scale[32 * q : 32 * q + 16].bitcast(I32), in_=w_scales[:, 4 * q : 4 * q + 4, :].bitcast(I32)
             )
         nc.scalar.activation(out=warmed[:], in_=warm[:], func=RELU)
 
         pairs = [(a, u) for a in range(PASSES) for u in range(2)]
-        cuts = {0: [0, 512, T], 7: [0, 640, 896, T]}
+        cuts = {7: [0, 640, 896, T]}
         raw = []
         for i, (a, u) in enumerate(pairs):
             x = keep.tile([P, 2, T], F32, name=f"x{i}")
@@ -56,13 +55,14 @@ def tile_picked_pick_lin_relu2_srt_e_kernel(tc, xT, w_words, w_scales, b, offs, 
             edges = cuts.get(i, [0, T])
             for c, (lo, hi) in enumerate(zip(edges[:-1], edges[1:])):
                 nc.sync.dma_start(out=x[:, :, lo:hi], in_=x_rows[a][:, 2 * u : 2 * u + 2, lo:hi])
-                if i == 0 and c == 0:
+                if i == 0:
                     nc.sync.dma_start(offsets[:], offs)
-            if i >= 6:
-                some = slice(2 * (i - 6), 2 * (i - 5))
-                nc.sync.dma_start(
-                    out=w_codes[:, some].bitcast(I32), in_=w_words[some].rearrange("a p n r -> p a (n r)").bitcast(I32)
-                )
+                if i == 7 and c > 0:
+                    some = slice(2 * c - 2, 2 * c)
+                    nc.sync.dma_start(
+                        out=w_codes[:, some].bitcast(I32),
+                        in_=w_words[some].rearrange("a p n r -> p a (n r)").bitcast(I32),
+                    )
 
         acc = []
         for h in range(4):
@@ -70,13 +70,13 @@ def tile_picked_pick_lin_relu2_srt_e_kernel(tc, xT, w_words, w_scales, b, offs, 
             acc.append(bank)
 
         plan = {
-            0: [("s", 0, 192), ("v", 192, 512), ("s", 512, 704), ("v", 704, T)],
+            0: [("s", 0, 384), ("g", 384, 576), ("v", 576, T)],
             6: [("s", 0, 768), ("g", 768, T)],
-            7: [("s", 0, 640), ("s", 640, 704), ("g", 704, 896), ("v", 896, T)],
+            7: [("s", 0, 640), ("g", 640, 896), ("s", 896, 960), ("v", 960, T)],
         }
         for i, (a, u) in enumerate(pairs):
             pair = keep.tile([P, T, 2], BF16, name=f"pair{i}")
-            for engine, lo, hi in plan.get(i, [("s", 0, 640), ("g", 640, T)]):
+            for engine, lo, hi in plan.get(i, [("s", 0, 576), ("g", 576, T)]):
                 src = raw[i][:, :, lo:hi].rearrange("p e t -> p t e")
                 if engine == "s":
                     nc.scalar.copy(out=pair[:, lo:hi, :], in_=src)
@@ -138,7 +138,7 @@ def tile_picked_pick_lin_relu2_srt_e_kernel(tc, xT, w_words, w_scales, b, offs, 
                     nc.tensor.matmul_mx(
                         out=acc[h][:, : hi - lo],
                         lhsT=w_codes[:, a, :].bitcast(FP8X4),
-                        lhsT_scale=w_scale[:, a, :],
+                        lhsT_scale=w_scale[4 * a : P, :],
                         rhs=codes[:, lo:hi].bitcast(FP8X4),
                         rhs_scale=scale[:, lo:hi],
                         start=(a == 0),
@@ -149,7 +149,7 @@ def tile_picked_pick_lin_relu2_srt_e_kernel(tc, xT, w_words, w_scales, b, offs, 
             relu = keep.tile([P, hi - lo], F32, name=f"relu{h}")
             y = keep.tile([P, hi - lo], F32, name=f"y{h}")
             total = acc[h][:, : hi - lo]
-            if h % 2 == 1:
+            if h in (1, 2):
                 nc.vector.tensor_scalar(out=relu[:], in0=total, scalar1=bias[:], scalar2=0.0, op0=ADD, op1=MAX)
                 nc.vector.tensor_tensor(out=y[:], in0=relu[:], in1=relu[:], op=MULT)
             else:

from contextlib import ExitStack

import concourse.mybir as mybir

K, T, S, N = 2048, 1024, 512, 128
FLOPS = 2 * K * S * N

F32 = mybir.dt.float32
BF16 = mybir.dt.bfloat16
I32 = mybir.dt.int32
U32 = mybir.dt.uint32
U16 = mybir.dt.uint16
U8 = mybir.dt.uint8
FP8X4 = mybir.dt.float8_e4m3fn_x4
RELU = mybir.ActivationFunctionType.Relu
SQUARE = mybir.ActivationFunctionType.Square
ADD, MAX, MULT = mybir.AluOpType.add, mybir.AluOpType.max, mybir.AluOpType.mult

P = 128
PASSES = K // 512
PIECES = [(0, 128), (128, 384), (384, 512)]
GROUPS = [(0, 128), (128, 256), (256, 384), (384, 512)]


def tile_picked_pick_lin_relu2_srt_e_kernel(tc, xT, w_words, w_scales, b, offs, out):
    nc = tc.nc
    x_rows = xT.rearrange("(a p j) t -> a p j t", p=P, j=4)

    with ExitStack() as ctx:
        keep = ctx.enter_context(tc.tile_pool(name="keep", bufs=1))
        psum = ctx.enter_context(tc.psum_pool(name="psum", bufs=1))

        offsets = keep.tile([P, S // 16], U16, name="offsets")
        bias = keep.tile([P, 1], F32, name="bias")
        w_codes = keep.tile([P, PASSES, N], U32, align_bytes=64, name="w_codes")
        w_scale = keep.tile([P, N], U8, align_bytes=64, name="w_scale")
        warm = keep.tile([P, 1], F32, name="warm")
        warmed = keep.tile([P, 1], F32, name="warmed")

        nc.vector.memset(w_scale[:].bitcast(I32), 0)
        nc.vector.memset(warm[:], 0.0)
        nc.scalar.dma_start(out=bias[:], in_=b)
        for q in range(4):
            nc.scalar.dma_start(
                out=w_scale[32 * q : 32 * q + 16].bitcast(I32), in_=w_scales[:, 4 * q : 4 * q + 4, :].bitcast(I32)
            )
        nc.scalar.activation(out=warmed[:], in_=warm[:], func=RELU)

        pairs = [(a, u) for a in range(PASSES) for u in range(2)]
        cuts = {7: [0, 640, 896, T]}
        raw = []
        for i, (a, u) in enumerate(pairs):
            x = keep.tile([P, 2, T], F32, name=f"x{i}")
            raw.append(x)
            edges = cuts.get(i, [0, T])
            for c, (lo, hi) in enumerate(zip(edges[:-1], edges[1:])):
                nc.sync.dma_start(out=x[:, :, lo:hi], in_=x_rows[a][:, 2 * u : 2 * u + 2, lo:hi])
                if i == 0:
                    nc.sync.dma_start(offsets[:], offs)
                if i == 7 and c > 0:
                    some = slice(2 * c - 2, 2 * c)
                    nc.sync.dma_start(
                        out=w_codes[:, some].bitcast(I32),
                        in_=w_words[some].rearrange("a p n r -> p a (n r)").bitcast(I32),
                    )

        acc = []
        for h in range(4):
            bank = psum.tile([P, 512], F32, name=f"acc{h}")
            acc.append(bank)

        plan = {
            0: [("s", 0, 384), ("g", 384, 576), ("v", 576, T)],
            6: [("s", 0, 768), ("g", 768, T)],
            7: [("s", 0, 640), ("g", 640, 896), ("s", 896, 960), ("v", 960, T)],
        }
        for i, (a, u) in enumerate(pairs):
            pair = keep.tile([P, T, 2], BF16, name=f"pair{i}")
            for engine, lo, hi in plan.get(i, [("s", 0, 576), ("g", 576, T)]):
                src = raw[i][:, :, lo:hi].rearrange("p e t -> p t e")
                if engine == "s":
                    nc.scalar.copy(out=pair[:, lo:hi, :], in_=src)
                elif engine == "g":
                    nc.gpsimd.tensor_scalar(
                        out=pair[:, lo:hi, :], in0=src, scalar1=1.0, scalar2=0.0, op0=MULT, op1=ADD
                    )
                else:
                    nc.vector.tensor_copy(out=pair[:, lo:hi, :], in_=src)
            window = pair[:].rearrange("p t e -> p (t e)").bitcast(U32)
            if u == 0:
                gathered = keep.tile([P, 2, S, 2], BF16, align_bytes=64, name=f"gathered{a}")
                grouped = keep.tile([P, S, 4], BF16, align_bytes=64, name=f"grouped{a}")
                codes = keep.tile([P, S], U32, align_bytes=64, name=f"codes{a}")
                scale = keep.tile([P, S], U8, align_bytes=64, name=f"scale{a}")
            words = gathered[:, u].rearrange("p s e -> p (s e)").bitcast(U32)
            flat = grouped[:].rearrange("p s k -> p (s k)")
            last = a == PASSES - 1

            def gather(lo, hi):
                nc.vector.tensor_copy(
                    out=words[:, lo:hi],
                    in_=window[:, 0 : T - S + hi].indirect(offsets[:, lo // 16 : hi // 16]),
                )

            both = flat.bitcast(F32).rearrange("p (s u) -> p s u", u=2)
            apart = gathered[:].rearrange("p u s e -> p (u s e)").bitcast(F32).rearrange("p (u s) -> p s u", u=2)

            def interleave(lo, hi):
                nc.vector.tensor_copy(out=both[:, lo:hi], in_=apart[:, lo:hi])

            def quantise(lo, hi):
                nc.vector.quantize_mx(
                    out=codes[:, lo:hi].bitcast(FP8X4), scales=scale[:, lo:hi], in_=flat[:, 4 * lo : 4 * hi]
                )

            if i < 7:
                halves = [(0, 256), (256, 512)] if i == 5 else [(0, 512)]
                for lo, hi in halves:
                    gather(lo, hi)
                if u == 1:
                    for lo, hi in halves:
                        interleave(lo, hi)
                    for lo, hi in halves:
                        quantise(lo, hi)
            else:
                gather(*PIECES[0])
                gather(*PIECES[1])
                lo, hi = PIECES[1]
                nc.scalar.copy(out=both[:, lo:hi], in_=apart[:, lo:hi])
                interleave(*PIECES[0])
                gather(*PIECES[2])
                quantise(*PIECES[0])
                interleave(*PIECES[2])
                quantise(*PIECES[1])
                quantise(*PIECES[2])
            if u == 1:
                for h, (lo, hi) in enumerate(GROUPS):
                    nc.tensor.matmul_mx(
                        out=acc[h][:, : hi - lo],
                        lhsT=w_codes[:, a, :].bitcast(FP8X4),
                        lhsT_scale=w_scale[4 * a : P, :],
                        rhs=codes[:, lo:hi].bitcast(FP8X4),
                        rhs_scale=scale[:, lo:hi],
                        start=(a == 0),
                        stop=last,
                    )

        for h, (lo, hi) in enumerate(GROUPS):
            relu = keep.tile([P, hi - lo], F32, name=f"relu{h}")
            y = keep.tile([P, hi - lo], F32, name=f"y{h}")
            total = acc[h][:, : hi - lo]
            if h in (1, 2):
                nc.vector.tensor_scalar(out=relu[:], in0=total, scalar1=bias[:], scalar2=0.0, op0=ADD, op1=MAX)
                nc.vector.tensor_tensor(out=y[:], in0=relu[:], in1=relu[:], op=MULT)
            else:
                nc.scalar.activation(out=relu[:], in_=total, func=RELU, bias=bias[:])
                nc.scalar.activation(out=y[:], in_=relu[:], func=SQUARE)
            nc.sync.dma_start(out=out[:, lo:hi], in_=y[:])
